import numpy as np
import ml_dtypes


def mxq(x, axis, fmt="e4m3"):
    dtype, down = {"e4m3": (ml_dtypes.float8_e4m3fn, 7), "e5m2": (ml_dtypes.float8_e5m2, 14)}[fmt]
    v = np.moveaxis(np.asarray(x, np.float32).astype(ml_dtypes.bfloat16).astype(np.float64), axis, -1)
    blocks = v.reshape(v.shape[:-1] + (-1, 32))
    amax = np.abs(blocks).max(-1, keepdims=True)
    byte = np.maximum(np.where(amax > 0, np.frexp(amax)[1] - 1 + 127, 0) - down, 1)
    scale = np.exp2(byte - 127.0)
    codes = (blocks / scale).astype(np.float32).astype(dtype).astype(np.float64)
    return np.moveaxis((codes * scale).reshape(v.shape), -1, axis)


WIDE = False


def mx_kscale(k):
    if not WIDE:
        return np.ones(k)
    levels = np.array([10, -10, 5, -5, 0])
    if k % 512:
        return np.exp2(np.random.permutation(np.resize(levels, k // 32))).repeat(32)
    a = np.empty((k // 512, 16))
    for p in range(k // 512):
        a[p, :8] = np.random.permutation(np.resize(levels, 8))
        for g in range(8):
            far = levels[np.abs(levels - a[p, g]) >= 10]
            a[p, g + 8] = far[np.random.randint(len(far))]
    return np.exp2(a.ravel()).repeat(32)


def f64(x):
    return np.asarray(x).astype(np.float64)


def striped(idx):
    return np.tile(idx.reshape(-1, 16).T, (8, 1)).astype(np.uint16)


def unstriped(offs):
    return offs[:16].T.reshape(-1).astype(np.int64)


E2M1 = np.array([0.0, 0.5, 1.0, 1.5, 2.0, 3.0, 4.0, 6.0, -0.0, -0.5, -1.0, -1.5, -2.0, -3.0, -4.0, -6.0])


def pack_weight(w, fmt):
    k, n = w.shape
    w = f64(np.asarray(w, np.float32).astype(ml_dtypes.bfloat16)).reshape(k // 32, 32, n)
    amax = np.abs(w).max(1)
    if fmt == "e4m3":
        byte = np.frexp(amax)[1] - 1 + 127 - 7
    else:
        mant, ex = np.frexp(amax / 6.0)
        byte = np.where(mant > 0.5, ex, ex - 1) + 127
    byte = np.clip(np.where(amax > 0, byte, 1), 1, 254)
    scaled = (w * np.exp2(127.0 - byte)[:, None, :]).reshape(k, n).astype(np.float32)
    by_word = np.ascontiguousarray(scaled.reshape(k // 512, 128, 4, n).transpose(0, 1, 3, 2))
    if fmt == "e4m3":
        words = by_word.astype(ml_dtypes.float8_e4m3fn).view(np.uint8)
    else:
        c = by_word.astype(ml_dtypes.float4_e2m1fn).view(np.uint8) & 0xF
        words = (c[..., 0::2] | (c[..., 1::2] << 4)).reshape(k // 512, 128, 2 * n)
    return np.ascontiguousarray(words), np.ascontiguousarray(byte.astype(np.uint8).reshape(k // 512, 16, n))


def unpack_weight(words, scales, fmt):
    g, _, n = scales.shape
    words = np.ascontiguousarray(words).reshape(g, 128, n, -1)
    if fmt == "e4m3":
        vals = words.view(ml_dtypes.float8_e4m3fn).astype(np.float64)
    else:
        nib = np.empty((g, 128, n, 4), np.uint8)
        nib[..., 0::2] = words & 0xF
        nib[..., 1::2] = words >> 4
        vals = E2M1[nib]
    vals = vals * np.repeat(np.exp2(scales.astype(np.float64) - 127.0), 8, axis=1)[..., None]
    return vals.transpose(0, 1, 3, 2).reshape(g * 512, n)


def gelu(v):
    return 0.5 * v * (1.0 + np.tanh(np.sqrt(2.0 / np.pi) * (v + 0.044715 * v**3)))


def often(T, S):
    return np.random.permutation(T)[(T * np.random.uniform(0, 1, S) ** 4).astype(np.int64)]


def bf(x):
    return np.asarray(x, np.float32).astype(ml_dtypes.bfloat16)


def planes(Y):
    n, m = Y.shape
    b = f64(bf(Y)).reshape(n // 32, 32, m)
    amax = np.abs(b).max(1)
    byte = np.clip(np.where(amax > 0, np.frexp(amax)[1] - 1 + 127 - 7, 1), 1, 254)
    codes = (b * np.exp2(127.0 - byte)[:, None, :]).reshape(n, m).astype(np.float32).astype(ml_dtypes.float8_e4m3fn).view(np.uint8)
    words = codes.reshape(n // 512, 128, 4, m).transpose(0, 1, 3, 2)
    return np.ascontiguousarray(words), np.ascontiguousarray(byte.astype(np.uint8).reshape(n // 512, 16, m))


K, K2, T, S, H, P, N = 1024, 512, 2048, 1024, 1024, 512, 1024

def setup_inputs():
    n = np.random.standard_normal
    s = mx_kscale(K)[:, None]
    s2 = mx_kscale(K2)[:, None]
    u = mx_kscale(H)[:, None]
    size = np.exp(0.8 * n(N))
    d = {}
    d["tab_words"], d["tab_scales"] = pack_weight(n((K, T)) * s, "e4m3")
    d["tab2_words"], d["tab2_scales"] = pack_weight(n((K2, T)) * s2, "e4m3")
    d["tab3_words"], d["tab3_scales"] = pack_weight(n((K2, T)) * s2, "e4m3")
    d["offs"] = striped(np.random.permutation(T)[:S])
    d["offs2"] = striped(np.random.permutation(T)[:S])
    d["offs3"] = striped(np.random.permutation(T)[:S])
    d["pos1"] = striped(np.random.permutation(S)[:P])
    d["pos2"] = striped(often(S, P))
    d["pos3"] = striped(often(S, P))
    d["w1"] = (n((K, H)) / s * u.T / K ** 0.5).astype(np.float32)
    d["w2_words"], d["w2_scales"] = pack_weight(n((K2, H)) / s2 * u.T / K2 ** 0.5, "e2m1")
    d["w3_words"], d["w3_scales"] = pack_weight(n((K2, H)) / s2 * u.T / K2 ** 0.5, "e4m3")
    d["w4"] = (1.5 * n((H, N)) / u * size / H ** 0.5).astype(np.float32)
    d["bias"] = (0.6 * n(N) * size).astype(np.float32)
    return d

def reference(tab_words, tab_scales, tab2_words, tab2_scales, tab3_words, tab3_scales,
              offs, offs2, offs3, pos1, pos2, pos3,
              w1, w2_words, w2_scales, w3_words, w3_scales, w4, bias):
    v = unpack_weight(tab_words, tab_scales, "e4m3")[:, unstriped(offs)]
    v2 = unpack_weight(tab2_words, tab2_scales, "e4m3")[:, unstriped(offs2)]
    v3 = unpack_weight(tab3_words, tab3_scales, "e4m3")[:, unstriped(offs3)]
    a = mxq(f64(w1), 0, "e4m3").T @ v
    b = unpack_weight(w2_words, w2_scales, "e2m1").T @ v2
    e = unpack_weight(w3_words, w3_scales, "e4m3").T @ v3
    x1 = a[:, unstriped(pos1)]
    x2 = b[:, unstriped(pos2)]
    x3 = e[:, unstriped(pos3)]
    z = np.maximum(np.minimum(x1, x2), np.minimum(x3, np.maximum(x1, x2)))
    y = (mxq(f64(w4), 0, "e4m3").T @ mxq(z, 0, "e4m3")) + f64(bias)[:, None]
    words, scales = planes(y)
    return y, words, scales

@@ -1,0 +1,268 @@
+from contextlib import ExitStack
+
+import concourse.mybir as mybir
+
+K, K2, T, S, H, W, N = 1024, 512, 2048, 1024, 1024, 512, 1024
+FLOPS = 2 * (K + 2 * K2) * H * S + 2 * H * N * W
+
+F32 = mybir.dt.float32
+BF16 = mybir.dt.bfloat16
+I32 = mybir.dt.int32
+U32 = mybir.dt.uint32
+U16 = mybir.dt.uint16
+U8 = mybir.dt.uint8
+FP8X4 = mybir.dt.float8_e4m3fn_x4
+FP4X4 = mybir.dt.float4_e2m1fn_x4
+MIN = mybir.AluOpType.min
+MAX = mybir.AluOpType.max
+ADD = mybir.AluOpType.add
+IDENTITY = mybir.ActivationFunctionType.Identity
+
+P = 128
+PACK = 4
+GROUP = P * PACK
+BANK = 512
+BANKS = 8
+HALF = W // 2
+
+
+def tile_list_airdata_median_vote_kernel(
+    tc, tab_words, tab_scales, tab2_words, tab2_scales, tab3_words, tab3_scales,
+    offs, offs2, offs3, pos1, pos2, pos3,
+    w1, w2_words, w2_scales, w3_words, w3_scales, w4, bias,
+    out_0, out_1, out_2,
+):
+    nc = tc.nc
+    with ExitStack() as ctx:
+        lists = ctx.enter_context(tc.tile_pool(name="lists", bufs=1))
+        keep = ctx.enter_context(tc.tile_pool(name="keep", bufs=1))
+        raw_pool = ctx.enter_context(tc.tile_pool(name="raw", bufs=3))
+        stage = ctx.enter_context(tc.tile_pool(name="stage", bufs=2))
+        rows = ctx.enter_context(tc.tile_pool(name="rows", bufs=4))
+        psum = ctx.enter_context(tc.psum_pool(name="psum", bufs=1))
+
+        def load_list(name, src):
+            tile = lists.tile(list(src.shape), U16, name=name)
+            nc.sync.dma_start(tile[:], src)
+            return tile
+
+        def words_view(ap):
+            return ap.rearrange("p c i -> p (c i)").bitcast(I32)
+
+        def load_words(name, src):
+            tile = keep.tile([P, src.shape[1]], U32, name=name, align_bytes=64)
+            nc.sync.dma_start(tile[:].bitcast(I32), words_view(src))
+            return tile
+
+        def zeroed_plane(name, width, engine):
+            tile = keep.tile([P, width], U8, name=name, align_bytes=64)
+            engine.memset(tile[:].bitcast(I32), 0)
+            return tile
+
+        def load_scales(tile, src, first_row, queue):
+            passes = src.shape[0]
+            for q in range(4):
+                p0 = 32 * q + first_row
+                queue.dma_start(tile[p0 : p0 + 4 * passes, :].bitcast(I32), src[:, 4 * q : 4 * q + 4, :].bitcast(I32))
+
+        def gather(name, table, offsets, dtype):
+            tile = keep.tile([P, S], dtype, name=name, align_bytes=64)
+            nc.vector.tensor_copy(tile[:], table[:].indirect(offsets[:]))
+            return tile
+
+        tab2_plane = zeroed_plane("tab2_plane", T, nc.vector)
+        tab3_plane = zeroed_plane("tab3_plane", T, nc.vector)
+        w23_plane = zeroed_plane("w23_plane", H, nc.vector)
+        tab_plane = zeroed_plane("tab_plane", T, nc.vector)
+
+        idx2 = load_list("idx2", offs2)
+        load_scales(tab2_plane, tab2_scales, 0, nc.sync)
+        tab2_w = load_words("tab2_w", tab2_words[0])
+        idx3 = load_list("idx3", offs3)
+        tab3_w = load_words("tab3_w", tab3_words[0])
+        load_scales(tab3_plane, tab3_scales, 0, nc.sync)
+        w2_raw = keep.tile([P, 2 * H], U8, name="w2_raw", align_bytes=64)
+        nc.sync.dma_start(w2_raw[:].bitcast(I32), w2_words[0].bitcast(I32))
+        w3_raw = load_words("w3_raw", w3_words[0])
+        load_scales(w23_plane, w2_scales, 0, nc.sync)
+        load_scales(w23_plane, w3_scales, 4, nc.sync)
+
+        def load_weight(w, a, g):
+            raw = raw_pool.tile([P, PACK, GROUP], F32, name="raw")
+            src = w[a * GROUP : (a + 1) * GROUP, g * GROUP : (g + 1) * GROUP]
+            nc.sync.dma_start(raw[:], src.rearrange("(p j) c -> p j c", j=PACK))
+            return raw
+
+        def quantize(name, grouped, width):
+            codes = keep.tile([P, width], U32, name=name + "_codes", align_bytes=64)
+            plane = keep.tile([P, width], U8, name=name + "_plane", align_bytes=64)
+            nc.vector.quantize_mx(out=codes[:].bitcast(FP8X4), scales=plane[:], in_=grouped)
+            return codes, plane
+
+        def quantize_weight(name, raw):
+            grouped = stage.tile([P, PACK * GROUP], BF16, name="grouped", align_bytes=64)
+            nc.scalar.copy(
+                grouped[:].rearrange("p (t m j) -> p m j t", t=PACK, j=PACK),
+                raw[:].rearrange("p j (m t) -> p m j t", t=PACK),
+            )
+            return quantize(name, grouped[:], GROUP)
+
+        w1_raw = {(a, 0): load_weight(w1, a, 0) for a in range(2)}
+        idx = load_list("idx", offs)
+        tab_w = [load_words("tab_w%d" % a, tab_words[a]) for a in range(2)]
+        load_scales(tab_plane, tab_scales, 0, nc.sync)
+        p2 = load_list("p2", pos2)
+        p3 = load_list("p3", pos3)
+        p1 = load_list("p1", pos1)
+        bias_sb = keep.tile([P, 2, PACK], F32, name="bias_sb")
+        nc.sync.dma_start(bias_sb[:], bias.rearrange("(g p t) -> p g t", p=P, t=PACK))
+
+        v2_plane = gather("v2_plane", tab2_plane, idx2, U8)
+        v2_w = gather("v2_w", tab2_w, idx2, U32)
+        v3_plane = gather("v3_plane", tab3_plane, idx3, U8)
+        v3_w = gather("v3_w", tab3_w, idx3, U32)
+        w2_dealt = keep.tile([P, 2 * H], U8, name="w2_dealt", align_bytes=64)
+        nc.vector.tensor_copy(
+            w2_dealt[:].rearrange("p (g t m b) -> p g t m b", g=2, t=PACK, b=2),
+            w2_raw[:].rearrange("p (g m t b) -> p g t m b", g=2, t=PACK, b=2),
+        )
+        w23_dealt = keep.tile([P, H], U8, name="w23_dealt", align_bytes=64)
+        nc.vector.tensor_copy(
+            w23_dealt[:].rearrange("p (g t m) -> p g t m", g=2, t=PACK),
+            w23_plane[:].rearrange("p (g m t) -> p g t m", g=2, t=PACK),
+        )
+        w3_dealt = keep.tile([P, H], U32, name="w3_dealt", align_bytes=64)
+        nc.vector.tensor_copy(
+            w3_dealt[:].bitcast(I32).rearrange("p (g t m) -> p g m t", g=2, t=PACK),
+            w3_raw[:].bitcast(I32).rearrange("p (g m t) -> p g m t", g=2, t=PACK),
+        )
+        v_w = [gather("v_w%d" % a, tab_w[a], idx, U32) for a in range(2)]
+        v_plane = gather("v_plane", tab_plane, idx, U8)
+
+        bank_count = [0]
+
+        def next_bank():
+            tile = psum.tile([P, BANK], F32, name="bank%d" % (bank_count[0] % BANKS))
+            bank_count.append(bank_count.pop() + 1)
+            return tile
+
+        def first_stage(name, passes):
+            result = rows.tile([P, S], F32, name=name)
+            for c0 in range(0, S, BANK):
+                cols = slice(c0, c0 + BANK)
+                bank = next_bank()
+                for i, (lhsT, lhsT_scale, words, plane, row) in enumerate(passes):
+                    nc.tensor.matmul_mx(
+                        out=bank[:], lhsT=lhsT, lhsT_scale=lhsT_scale,
+                        rhs=words[:, cols].bitcast(FP8X4), rhs_scale=plane[row:P, cols],
+                        start=(i == 0), stop=(i == len(passes) - 1),
+                    )
+                nc.scalar.copy(result[:, cols], bank[:])
+            return result
+
+        def rows_b(g, t):
+            c = (g * PACK + t) * P
+            return first_stage("b", [(w2_dealt[:, 2 * c : 2 * (c + P)].bitcast(FP4X4), w23_dealt[:, c : c + P], v2_w, v2_plane, 0)])
+
+        def rows_e(g, t):
+            c = (g * PACK + t) * P
+            return first_stage("e", [(w3_dealt[:, c : c + P].bitcast(FP8X4), w23_dealt[4:P, c : c + P], v3_w, v3_plane, 0)])
+
+        def rows_a(w1_q, t):
+            cols = slice(t * P, (t + 1) * P)
+            return first_stage("a", [(w1_q[a][0][:, cols].bitcast(FP8X4), w1_q[a][1][:, cols], v_w[a], v_plane, 4 * a) for a in range(2)])
+
+        x1 = keep.tile([P, PACK * W], F32, name="x1")
+        x2 = keep.tile([P, PACK * W], F32, name="x2")
+        x3 = keep.tile([P, PACK * W], F32, name="x3")
+        low = keep.tile([P, PACK * W], F32, name="low")
+        high = keep.tile([P, PACK * W], F32, name="high")
+
+        def pick(x, at, source, positions, j0, width):
+            nc.vector.tensor_copy(x[:, at : at + width], source[:].indirect(positions[:, j0 // 16 : (j0 + width) // 16]))
+
+        def vote(name, a, b, e, base, j0, width):
+            for t in range(PACK):
+                pick(x2, base + t * width, b[t], p2, j0, width)
+                pick(x3, base + t * width, e[t], p3, j0, width)
+                pick(x1, base + t * width, a[t], p1, j0, width)
+                if t % 2 == 1:
+                    cols = slice(base + (t - 1) * width, base + (t + 1) * width)
+                    nc.vector.tensor_tensor(high[:, cols], x1[:, cols], x2[:, cols], MAX)
+                    nc.vector.tensor_tensor(low[:, cols], x1[:, cols], x2[:, cols], MIN)
+                    nc.vector.tensor_tensor(high[:, cols], high[:, cols], x3[:, cols], MIN)
+            cols = slice(base, base + PACK * width)
+            z = stage.tile([P, PACK * width], BF16, name="z", align_bytes=64)
+            nc.vector.tensor_tensor(
+                z[:].rearrange("p (c i t) -> p c t i", i=4, t=PACK),
+                low[:, cols].rearrange("p (t c i) -> p c t i", i=4, t=PACK),
+                high[:, cols].rearrange("p (t c i) -> p c t i", i=4, t=PACK),
+                MAX,
+            )
+            return quantize(name, z[:], width)
+
+        w1_q0 = [quantize_weight("w1_%d0" % a, w1_raw[a, 0]) for a in range(2)]
+        a0, b0, e0 = [], [], []
+        for t in range(2):
+            b0.append(rows_b(0, t))
+            e0.append(rows_e(0, t))
+        w1_q1 = [quantize_weight("w1_01", load_weight(w1, 0, 1))]
+        a0.extend(rows_a(w1_q0, t) for t in range(2))
+        w1_q1.append(quantize_weight("w1_11", load_weight(w1, 1, 1)))
+        for t in range(2, PACK):
+            b0.append(rows_b(0, t))
+            e0.append(rows_e(0, t))
+            a0.append(rows_a(w1_q0, t))
+        z0 = vote("z0", a0, b0, e0, 0, 0, W)
+
+        a1, b1, e1 = [], [], []
+        w4_q = {}
+        for t in range(PACK):
+            if t < 3:
+                w4_q[t // 2, t % 2] = quantize_weight("w4_%d" % t, load_weight(w4, t // 2, t % 2))
+            b1.append(rows_b(1, t))
+            e1.append(rows_e(1, t))
+            a1.append(rows_a(w1_q1, t))
+        w4_q[1, 1] = quantize_weight("w4_3", load_weight(w4, 1, 1))
+
+        y_codes = keep.tile([P, 2, W], U32, name="y_codes", align_bytes=64)
+        y_plane = keep.tile([P, 2, W], U8, name="y_plane", align_bytes=64)
+
+        def last_pass(bank, a, g, t, codes, plane):
+            cols = slice(t * P, (t + 1) * P)
+            nc.tensor.matmul_mx(
+                out=bank[:, :HALF], lhsT=w4_q[a, g][0][:, cols].bitcast(FP8X4), lhsT_scale=w4_q[a, g][1][:, cols],
+                rhs=codes.bitcast(FP8X4), rhs_scale=plane, start=(a == 0), stop=(a == 1),
+            )
+
+        for h in range(2):
+            cols = slice(h * HALF, (h + 1) * HALF)
+            banks = {}
+            for g in range(2):
+                for t in range(PACK):
+                    banks[g, t] = next_bank()
+                    last_pass(banks[g, t], 0, g, t, z0[0][:, cols], z0[1][:, cols])
+            z1 = vote("z1_%d" % h, a1, b1, e1, 0, h * HALF, HALF)
+            for g in range(2):
+                y = raw_pool.tile([P, PACK, HALF], F32, name="raw")
+                for t in range(PACK):
+                    last_pass(banks[g, t], 1, g, t, z1[0][:], z1[1][:])
+                    if h == 1 and t % 2 == 1:
+                        nc.vector.tensor_scalar(y[:, t, :], banks[g, t][:, :HALF], bias_sb[:, g, t : t + 1], None, ADD)
+                    else:
+                        nc.scalar.activation(y[:, t, :], banks[g, t][:, :HALF], IDENTITY, bias=bias_sb[:, g, t : t + 1])
+                nc.sync.dma_start(out_0[g * GROUP : (g + 1) * GROUP, cols].rearrange("(p t) j -> p t j", t=PACK), y[:])
+                y_grouped = stage.tile([P, PACK * HALF], BF16, name="grouped", align_bytes=64)
+                dst = y_grouped[:].rearrange("p (c i t) -> p c t i", i=4, t=PACK)
+                src = y[:].rearrange("p t (c i) -> p c t i", i=4)
+                if h == 1:
+                    nc.vector.tensor_copy(dst, src)
+                else:
+                    nc.scalar.copy(dst, src)
+                nc.vector.quantize_mx(out=y_codes[:, g, cols].bitcast(FP8X4), scales=y_plane[:, g, cols], in_=y_grouped[:])
+                nc.sync.dma_start(words_view(out_1[g, :, cols, :]), y_codes[:, g, cols].bitcast(I32))
+        for q in range(4):
+            nc.scalar.dma_start(
+                out_2[:, 4 * q : 4 * q + 4, :].bitcast(I32).rearrange("g r c -> r g c"),
+                y_plane[32 * q : 32 * q + 4, :, :].bitcast(I32),
+            )

@@ -23,7 +23,7 @@ PACK = 4
 GROUP = P * PACK
 BANK = 512
 BANKS = 8
-HALF = W // 2
+PARTS = (256, 128, 128)
 
 
 def tile_list_airdata_median_vote_kernel(
@@ -36,108 +36,122 @@ def tile_list_airdata_median_vote_kernel(
     with ExitStack() as ctx:
         lists = ctx.enter_context(tc.tile_pool(name="lists", bufs=1))
         keep = ctx.enter_context(tc.tile_pool(name="keep", bufs=1))
-        raw_pool = ctx.enter_context(tc.tile_pool(name="raw", bufs=3))
+        raw_pool = ctx.enter_context(tc.tile_pool(name="raw", bufs=4))
+        late = ctx.enter_context(tc.tile_pool(name="late", bufs=4))
         stage = ctx.enter_context(tc.tile_pool(name="stage", bufs=2))
         rows = ctx.enter_context(tc.tile_pool(name="rows", bufs=4))
         psum = ctx.enter_context(tc.psum_pool(name="psum", bufs=1))
+        with tc.tile_pool(name="tables", bufs=1) as tables:
 
-        def load_list(name, src):
-            tile = lists.tile(list(src.shape), U16, name=name)
-            nc.sync.dma_start(tile[:], src)
-            return tile
+            def load_list(name, src):
+                tile = lists.tile(list(src.shape), U16, name=name)
+                nc.sync.dma_start(tile[:], src)
+                return tile
 
-        def words_view(ap):
-            return ap.rearrange("p c i -> p (c i)").bitcast(I32)
+            def words_view(ap):
+                return ap.rearrange("p c i -> p (c i)").bitcast(I32)
 
-        def load_words(name, src):
-            tile = keep.tile([P, src.shape[1]], U32, name=name, align_bytes=64)
-            nc.sync.dma_start(tile[:].bitcast(I32), words_view(src))
-            return tile
+            def load_words(name, src):
+                tile = tables.tile([P, src.shape[1]], U32, name=name, align_bytes=64)
+                nc.sync.dma_start(tile[:].bitcast(I32), words_view(src))
+                return tile
 
-        def zeroed_plane(name, width, engine):
-            tile = keep.tile([P, width], U8, name=name, align_bytes=64)
-            engine.memset(tile[:].bitcast(I32), 0)
-            return tile
+            def zeroed_plane(name, width, engine):
+                tile = tables.tile([P, width], U8, name=name, align_bytes=64)
+                engine.memset(tile[:].bitcast(I32), 0)
+                return tile
 
-        def load_scales(tile, src, first_row, queue):
-            passes = src.shape[0]
-            for q in range(4):
-                p0 = 32 * q + first_row
-                queue.dma_start(tile[p0 : p0 + 4 * passes, :].bitcast(I32), src[:, 4 * q : 4 * q + 4, :].bitcast(I32))
+            def load_scales(tile, src, first_row, queue):
+                passes = src.shape[0]
+                for q in range(4):
+                    p0 = 32 * q + first_row
+                    queue.dma_start(tile[p0 : p0 + 4 * passes, :].bitcast(I32), src[:, 4 * q : 4 * q + 4, :].bitcast(I32))
 
-        def gather(name, table, offsets, dtype):
-            tile = keep.tile([P, S], dtype, name=name, align_bytes=64)
-            nc.vector.tensor_copy(tile[:], table[:].indirect(offsets[:]))
-            return tile
+            def gather(name, table, offsets, dtype):
+                tile = keep.tile([P, S], dtype, name=name, align_bytes=64)
+                nc.vector.tensor_copy(tile[:], table[:].indirect(offsets[:]))
+                return tile
 
-        tab2_plane = zeroed_plane("tab2_plane", T, nc.vector)
-        tab3_plane = zeroed_plane("tab3_plane", T, nc.vector)
-        w23_plane = zeroed_plane("w23_plane", H, nc.vector)
-        tab_plane = zeroed_plane("tab_plane", T, nc.vector)
+            def load_w1(a, g):
+                raw = raw_pool.tile([P, PACK, GROUP], F32, name="raw")
+                src = w1[a * GROUP : (a + 1) * GROUP, g * GROUP : (g + 1) * GROUP]
+                nc.sync.dma_start(raw[:], src.rearrange("(p j) c -> p j c", j=PACK))
+                return raw
 
-        idx2 = load_list("idx2", offs2)
-        load_scales(tab2_plane, tab2_scales, 0, nc.sync)
-        tab2_w = load_words("tab2_w", tab2_words[0])
-        idx3 = load_list("idx3", offs3)
-        tab3_w = load_words("tab3_w", tab3_words[0])
-        load_scales(tab3_plane, tab3_scales, 0, nc.sync)
-        w2_raw = keep.tile([P, 2 * H], U8, name="w2_raw", align_bytes=64)
-        nc.sync.dma_start(w2_raw[:].bitcast(I32), w2_words[0].bitcast(I32))
-        w3_raw = load_words("w3_raw", w3_words[0])
-        load_scales(w23_plane, w2_scales, 0, nc.sync)
-        load_scales(w23_plane, w3_scales, 4, nc.sync)
+            def load_w4(a, g):
+                raw = late.tile([P, PACK, GROUP], F32, name="late")
+                src = w4[a * GROUP : (a + 1) * GROUP, g * GROUP : (g + 1) * GROUP].rearrange("(u j i) c -> j u i c", j=PACK, i=4)
+                for j in range(PACK):
+                    nc.sync.dma_start(raw[:, j, :], src[j])
+                return raw
 
-        def load_weight(w, a, g):
-            raw = raw_pool.tile([P, PACK, GROUP], F32, name="raw")
-            src = w[a * GROUP : (a + 1) * GROUP, g * GROUP : (g + 1) * GROUP]
-            nc.sync.dma_start(raw[:], src.rearrange("(p j) c -> p j c", j=PACK))
-            return raw
+            def quantize(name, grouped, width):
+                codes = keep.tile([P, width], U32, name=name + "_codes", align_bytes=64)
+                plane = keep.tile([P, width], U8, name=name + "_plane", align_bytes=64)
+                nc.vector.quantize_mx(out=codes[:].bitcast(FP8X4), scales=plane[:], in_=grouped)
+                return codes, plane
 
-        def quantize(name, grouped, width):
-            codes = keep.tile([P, width], U32, name=name + "_codes", align_bytes=64)
-            plane = keep.tile([P, width], U8, name=name + "_plane", align_bytes=64)
-            nc.vector.quantize_mx(out=codes[:].bitcast(FP8X4), scales=plane[:], in_=grouped)
-            return codes, plane
+            def quantize_w1(name, raw):
+                grouped = stage.tile([P, PACK * GROUP], BF16, name="grouped", align_bytes=64)
+                nc.scalar.copy(
+                    grouped[:].rearrange("p (t u i j) -> p u t j i", t=PACK, i=4, j=PACK),
+                    raw[:].rearrange("p j (u t i) -> p u t j i", t=PACK, i=4),
+                )
+                return quantize(name, grouped[:], GROUP)
 
-        def quantize_weight(name, raw):
-            grouped = stage.tile([P, PACK * GROUP], BF16, name="grouped", align_bytes=64)
-            nc.scalar.copy(
-                grouped[:].rearrange("p (t m j) -> p m j t", t=PACK, j=PACK),
-                raw[:].rearrange("p j (m t) -> p m j t", t=PACK),
-            )
-            return quantize(name, grouped[:], GROUP)
+            def quantize_w4(name, raw):
+                grouped = stage.tile([P, PACK * GROUP], BF16, name="grouped", align_bytes=64)
+                nc.scalar.copy(
+                    grouped[:].rearrange("p (t m j) -> p m j t", t=PACK, j=PACK),
+                    raw[:].rearrange("p j (m t) -> p m j t", t=PACK),
+                )
+                return quantize(name, grouped[:], GROUP)
 
-        w1_raw = {(a, 0): load_weight(w1, a, 0) for a in range(2)}
-        idx = load_list("idx", offs)
-        tab_w = [load_words("tab_w%d" % a, tab_words[a]) for a in range(2)]
-        load_scales(tab_plane, tab_scales, 0, nc.sync)
-        p2 = load_list("p2", pos2)
-        p3 = load_list("p3", pos3)
-        p1 = load_list("p1", pos1)
-        bias_sb = keep.tile([P, 2, PACK], F32, name="bias_sb")
-        nc.sync.dma_start(bias_sb[:], bias.rearrange("(g p t) -> p g t", p=P, t=PACK))
+            tab2_plane = zeroed_plane("tab2_plane", T, nc.vector)
+            tab3_plane = zeroed_plane("tab3_plane", T, nc.vector)
+            w23_plane = zeroed_plane("w23_plane", H, nc.vector)
+            tab_plane = zeroed_plane("tab_plane", T, nc.vector)
 
-        v2_plane = gather("v2_plane", tab2_plane, idx2, U8)
-        v2_w = gather("v2_w", tab2_w, idx2, U32)
-        v3_plane = gather("v3_plane", tab3_plane, idx3, U8)
-        v3_w = gather("v3_w", tab3_w, idx3, U32)
-        w2_dealt = keep.tile([P, 2 * H], U8, name="w2_dealt", align_bytes=64)
-        nc.vector.tensor_copy(
-            w2_dealt[:].rearrange("p (g t m b) -> p g t m b", g=2, t=PACK, b=2),
-            w2_raw[:].rearrange("p (g m t b) -> p g t m b", g=2, t=PACK, b=2),
-        )
-        w23_dealt = keep.tile([P, H], U8, name="w23_dealt", align_bytes=64)
-        nc.vector.tensor_copy(
-            w23_dealt[:].rearrange("p (g t m) -> p g t m", g=2, t=PACK),
-            w23_plane[:].rearrange("p (g m t) -> p g t m", g=2, t=PACK),
-        )
-        w3_dealt = keep.tile([P, H], U32, name="w3_dealt", align_bytes=64)
-        nc.vector.tensor_copy(
-            w3_dealt[:].bitcast(I32).rearrange("p (g t m) -> p g m t", g=2, t=PACK),
-            w3_raw[:].bitcast(I32).rearrange("p (g m t) -> p g m t", g=2, t=PACK),
-        )
-        v_w = [gather("v_w%d" % a, tab_w[a], idx, U32) for a in range(2)]
-        v_plane = gather("v_plane", tab_plane, idx, U8)
+            idx2 = load_list("idx2", offs2)
+            idx3 = load_list("idx3", offs3)
+            idx = load_list("idx", offs)
+            load_scales(tab2_plane, tab2_scales, 0, nc.sync)
+            tab2_w = load_words("tab2_w", tab2_words[0])
+            load_scales(tab3_plane, tab3_scales, 0, nc.sync)
+            w1_raw = [load_w1(0, 0)]
+            tab3_w = load_words("tab3_w", tab3_words[0])
+            w2_raw = tables.tile([P, 2 * H], U8, name="w2_raw", align_bytes=64)
+            nc.sync.dma_start(w2_raw[:].bitcast(I32), w2_words[0].bitcast(I32))
+            w3_raw = load_words("w3_raw", w3_words[0])
+            load_scales(w23_plane, w2_scales, 0, nc.sync)
+            load_scales(w23_plane, w3_scales, 4, nc.sync)
+            load_scales(tab_plane, tab_scales, 0, nc.sync)
+            w1_raw.append(load_w1(1, 0))
+            tab_w = [load_words("tab_w%d" % a, tab_words[a]) for a in range(2)]
+            p2 = load_list("p2", pos2)
+            p3 = load_list("p3", pos3)
+            p1 = load_list("p1", pos1)
+            bias_sb = keep.tile([P, 2, PACK], F32, name="bias_sb")
+            nc.sync.dma_start(bias_sb[:], bias.rearrange("(g p t) -> p g t", p=P, t=PACK))
+
+            v2_plane = gather("v2_plane", tab2_plane, idx2, U8)
+            v2_w = gather("v2_w", tab2_w, idx2, U32)
+            v3_plane = gather("v3_plane", tab3_plane, idx3, U8)
+            v3_w = gather("v3_w", tab3_w, idx3, U32)
+            def deal(name, raw, dtype, width, run):
+                dealt = keep.tile([P, width], dtype, name=name, align_bytes=64)
+                nc.vector.tensor_copy(
+                    dealt[:].bitcast(I32).rearrange("p (g t u h) -> p g u t h", g=2, t=PACK, h=run),
+                    raw[:].bitcast(I32).rearrange("p (g u t h) -> p g u t h", g=2, t=PACK, h=run),
+                )
+                return dealt
+
+            w2_dealt = deal("w2_dealt", w2_raw, U8, 2 * H, 2)
+            w3_dealt = deal("w3_dealt", w3_raw, U32, H, 4)
+            w23_dealt = deal("w23_dealt", w23_plane, U8, H, 1)
+            v_plane = gather("v_plane", tab_plane, idx, U8)
+            v_w = [gather("v_w%d" % a, tab_w[a], idx, U32) for a in range(2)]
+        picks = ctx.enter_context(tc.tile_pool(name="picks", bufs=1))
 
         bank_count = [0]
 
@@ -172,16 +186,14 @@ def tile_list_airdata_median_vote_kernel(
             cols = slice(t * P, (t + 1) * P)
             return first_stage("a", [(w1_q[a][0][:, cols].bitcast(FP8X4), w1_q[a][1][:, cols], v_w[a], v_plane, 4 * a) for a in range(2)])
 
-        x1 = keep.tile([P, PACK * W], F32, name="x1")
-        x2 = keep.tile([P, PACK * W], F32, name="x2")
-        x3 = keep.tile([P, PACK * W], F32, name="x3")
-        low = keep.tile([P, PACK * W], F32, name="low")
-        high = keep.tile([P, PACK * W], F32, name="high")
+        work = [picks.tile([P, PACK * W], F32, name="work%d" % i) for i in range(5)]
 
         def pick(x, at, source, positions, j0, width):
             nc.vector.tensor_copy(x[:, at : at + width], source[:].indirect(positions[:, j0 // 16 : (j0 + width) // 16]))
 
-        def vote(name, a, b, e, base, j0, width):
+        def vote(name, a, b, e, tiles, j0, width):
+            base = 0
+            x1, x2, x3, high, low = tiles
             for t in range(PACK):
                 pick(x2, base + t * width, b[t], p2, j0, width)
                 pick(x3, base + t * width, e[t], p3, j0, width)
@@ -201,29 +213,29 @@ def tile_list_airdata_median_vote_kernel(
             )
             return quantize(name, z[:], width)
 
-        w1_q0 = [quantize_weight("w1_%d0" % a, w1_raw[a, 0]) for a in range(2)]
+        w1_q0 = [quantize_w1("w1_%d0" % a, w1_raw[a]) for a in range(2)]
         a0, b0, e0 = [], [], []
         for t in range(2):
             b0.append(rows_b(0, t))
             e0.append(rows_e(0, t))
-        w1_q1 = [quantize_weight("w1_01", load_weight(w1, 0, 1))]
+        w1_q1 = [quantize_w1("w1_01", load_w1(0, 1))]
         a0.extend(rows_a(w1_q0, t) for t in range(2))
-        w1_q1.append(quantize_weight("w1_11", load_weight(w1, 1, 1)))
+        w1_q1.append(quantize_w1("w1_11", load_w1(1, 1)))
         for t in range(2, PACK):
             b0.append(rows_b(0, t))
             e0.append(rows_e(0, t))
             a0.append(rows_a(w1_q0, t))
-        z0 = vote("z0", a0, b0, e0, 0, 0, W)
+        z0 = vote("z0", a0, b0, e0, work, 0, W)
 
         a1, b1, e1 = [], [], []
         w4_q = {}
         for t in range(PACK):
             if t < 3:
-                w4_q[t // 2, t % 2] = quantize_weight("w4_%d" % t, load_weight(w4, t // 2, t % 2))
+                w4_q[t // 2, t % 2] = quantize_w4("w4_%d" % t, load_w4(t // 2, t % 2))
             b1.append(rows_b(1, t))
             e1.append(rows_e(1, t))
             a1.append(rows_a(w1_q1, t))
-        w4_q[1, 1] = quantize_weight("w4_3", load_weight(w4, 1, 1))
+        w4_q[1, 1] = quantize_w4("w4_3", load_w4(1, 1))
 
         y_codes = keep.tile([P, 2, W], U32, name="y_codes", align_bytes=64)
         y_plane = keep.tile([P, 2, W], U8, name="y_plane", align_bytes=64)
@@ -231,36 +243,40 @@ def tile_list_airdata_median_vote_kernel(
         def last_pass(bank, a, g, t, codes, plane):
             cols = slice(t * P, (t + 1) * P)
             nc.tensor.matmul_mx(
-                out=bank[:, :HALF], lhsT=w4_q[a, g][0][:, cols].bitcast(FP8X4), lhsT_scale=w4_q[a, g][1][:, cols],
+                out=bank, lhsT=w4_q[a, g][0][:, cols].bitcast(FP8X4), lhsT_scale=w4_q[a, g][1][:, cols],
                 rhs=codes.bitcast(FP8X4), rhs_scale=plane, start=(a == 0), stop=(a == 1),
             )
 
-        for h in range(2):
-            cols = slice(h * HALF, (h + 1) * HALF)
+        j0 = 0
+        for width in PARTS:
+            cols = slice(j0, j0 + width)
+            last = j0 + width == W
             banks = {}
             for g in range(2):
                 for t in range(PACK):
-                    banks[g, t] = next_bank()
+                    banks[g, t] = next_bank()[:, :width]
                     last_pass(banks[g, t], 0, g, t, z0[0][:, cols], z0[1][:, cols])
-            z1 = vote("z1_%d" % h, a1, b1, e1, 0, h * HALF, HALF)
+            z1 = vote("z1_%d" % j0, a1, b1, e1, work, j0, width)
+            work = [work[0], work[3], work[4], work[1], work[2]]
             for g in range(2):
-                y = raw_pool.tile([P, PACK, HALF], F32, name="raw")
+                y = late.tile([P, PACK, width], F32, name="late")
                 for t in range(PACK):
                     last_pass(banks[g, t], 1, g, t, z1[0][:], z1[1][:])
-                    if h == 1 and t % 2 == 1:
-                        nc.vector.tensor_scalar(y[:, t, :], banks[g, t][:, :HALF], bias_sb[:, g, t : t + 1], None, ADD)
+                    if last and t % 2 == 1:
+                        nc.vector.tensor_scalar(y[:, t, :], banks[g, t], bias_sb[:, g, t : t + 1], None, ADD)
                     else:
-                        nc.scalar.activation(y[:, t, :], banks[g, t][:, :HALF], IDENTITY, bias=bias_sb[:, g, t : t + 1])
+                        nc.scalar.activation(y[:, t, :], banks[g, t], IDENTITY, bias=bias_sb[:, g, t : t + 1])
                 nc.sync.dma_start(out_0[g * GROUP : (g + 1) * GROUP, cols].rearrange("(p t) j -> p t j", t=PACK), y[:])
-                y_grouped = stage.tile([P, PACK * HALF], BF16, name="grouped", align_bytes=64)
+                y_grouped = stage.tile([P, PACK * width], BF16, name="grouped", align_bytes=64)
                 dst = y_grouped[:].rearrange("p (c i t) -> p c t i", i=4, t=PACK)
                 src = y[:].rearrange("p t (c i) -> p c t i", i=4)
-                if h == 1:
+                if last:
                     nc.vector.tensor_copy(dst, src)
                 else:
                     nc.scalar.copy(dst, src)
                 nc.vector.quantize_mx(out=y_codes[:, g, cols].bitcast(FP8X4), scales=y_plane[:, g, cols], in_=y_grouped[:])
                 nc.sync.dma_start(words_view(out_1[g, :, cols, :]), y_codes[:, g, cols].bitcast(I32))
+            j0 = j0 + width
         for q in range(4):
             nc.scalar.dma_start(
                 out_2[:, 4 * q : 4 * q + 4, :].bitcast(I32).rearrange("g r c -> r g c"),

@@ -23,6 +23,7 @@ PACK = 4
 GROUP = P * PACK
 BANK = 512
 BANKS = 8
+ON_VECTOR = ["w1_10"]
 PARTS = (256, 128, 128)
 
 
@@ -53,7 +54,9 @@ def tile_list_airdata_median_vote_kernel(
 
             def load_words(name, src):
                 tile = tables.tile([P, src.shape[1]], U32, name=name, align_bytes=64)
-                nc.sync.dma_start(tile[:].bitcast(I32), words_view(src))
+                step = 1024
+                for c0 in range(0, src.shape[1], step):
+                    nc.sync.dma_start(tile[:, c0 : c0 + step].bitcast(I32), words_view(src[:, c0 : c0 + step, :]))
                 return tile
 
             def zeroed_plane(name, width, engine):
@@ -61,9 +64,9 @@ def tile_list_airdata_median_vote_kernel(
                 engine.memset(tile[:].bitcast(I32), 0)
                 return tile
 
-            def load_scales(tile, src, first_row, queue):
+            def load_scales(tile, src, first_row, queue, quadrants=range(4)):
                 passes = src.shape[0]
-                for q in range(4):
+                for q in quadrants:
                     p0 = 32 * q + first_row
                     queue.dma_start(tile[p0 : p0 + 4 * passes, :].bitcast(I32), src[:, 4 * q : 4 * q + 4, :].bitcast(I32))
 
@@ -72,10 +75,11 @@ def tile_list_airdata_median_vote_kernel(
                 nc.vector.tensor_copy(tile[:], table[:].indirect(offsets[:]))
                 return tile
 
-            def load_w1(a, g):
+            def load_w1(a, g, step=2):
                 raw = raw_pool.tile([P, PACK, GROUP], F32, name="raw")
                 src = w1[a * GROUP : (a + 1) * GROUP, g * GROUP : (g + 1) * GROUP]
-                nc.sync.dma_start(raw[:], src.rearrange("(p j) c -> p j c", j=PACK))
+                for j in range(0, PACK, step):
+                    nc.sync.dma_start(raw[:, j : j + step, :], src.rearrange("(p j) c -> p j c", j=PACK)[:, j : j + step, :])
                 return raw
 
             def load_w4(a, g):
@@ -92,16 +96,18 @@ def tile_list_airdata_median_vote_kernel(
                 return codes, plane
 
             def quantize_w1(name, raw):
+                copy = nc.vector.tensor_copy if name in ON_VECTOR else nc.scalar.copy
                 grouped = stage.tile([P, PACK * GROUP], BF16, name="grouped", align_bytes=64)
-                nc.scalar.copy(
+                copy(
                     grouped[:].rearrange("p (t u i j) -> p u t j i", t=PACK, i=4, j=PACK),
                     raw[:].rearrange("p j (u t i) -> p u t j i", t=PACK, i=4),
                 )
                 return quantize(name, grouped[:], GROUP)
 
             def quantize_w4(name, raw):
+                copy = nc.vector.tensor_copy if name in ON_VECTOR else nc.scalar.copy
                 grouped = stage.tile([P, PACK * GROUP], BF16, name="grouped", align_bytes=64)
-                nc.scalar.copy(
+                copy(
                     grouped[:].rearrange("p (t m j) -> p m j t", t=PACK, j=PACK),
                     raw[:].rearrange("p j (m t) -> p m j t", t=PACK),
                 )
@@ -112,24 +118,28 @@ def tile_list_airdata_median_vote_kernel(
             w23_plane = zeroed_plane("w23_plane", H, nc.vector)
             tab_plane = zeroed_plane("tab_plane", T, nc.vector)
 
+            w1_raw, tab_w = {}, {}
             idx2 = load_list("idx2", offs2)
             idx3 = load_list("idx3", offs3)
             idx = load_list("idx", offs)
             load_scales(tab2_plane, tab2_scales, 0, nc.sync)
             tab2_w = load_words("tab2_w", tab2_words[0])
             load_scales(tab3_plane, tab3_scales, 0, nc.sync)
-            w1_raw = [load_w1(0, 0)]
             tab3_w = load_words("tab3_w", tab3_words[0])
+            w1_raw[0, 0] = load_w1(0, 0, PACK)
+            load_scales(w23_plane, w2_scales, 0, nc.sync)
             w2_raw = tables.tile([P, 2 * H], U8, name="w2_raw", align_bytes=64)
             nc.sync.dma_start(w2_raw[:].bitcast(I32), w2_words[0].bitcast(I32))
             w3_raw = load_words("w3_raw", w3_words[0])
-            load_scales(w23_plane, w2_scales, 0, nc.sync)
             load_scales(w23_plane, w3_scales, 4, nc.sync)
             load_scales(tab_plane, tab_scales, 0, nc.sync)
-            w1_raw.append(load_w1(1, 0))
-            tab_w = [load_words("tab_w%d" % a, tab_words[a]) for a in range(2)]
+            tab_w[0] = load_words("tab_w0", tab_words[0])
+            w1_raw[1, 0] = load_w1(1, 0)
             p2 = load_list("p2", pos2)
             p3 = load_list("p3", pos3)
+            tab_w[1] = load_words("tab_w1", tab_words[1])
+            w1_raw[0, 1] = load_w1(0, 1)
+            w1_raw[1, 1] = load_w1(1, 1)
             p1 = load_list("p1", pos1)
             bias_sb = keep.tile([P, 2, PACK], F32, name="bias_sb")
             nc.sync.dma_start(bias_sb[:], bias.rearrange("(g p t) -> p g t", p=P, t=PACK))
@@ -213,14 +223,14 @@ def tile_list_airdata_median_vote_kernel(
             )
             return quantize(name, z[:], width)
 
-        w1_q0 = [quantize_w1("w1_%d0" % a, w1_raw[a]) for a in range(2)]
+        w1_q0 = [quantize_w1("w1_%d0" % a, w1_raw[a, 0]) for a in range(2)]
         a0, b0, e0 = [], [], []
         for t in range(2):
             b0.append(rows_b(0, t))
             e0.append(rows_e(0, t))
-        w1_q1 = [quantize_w1("w1_01", load_w1(0, 1))]
+        w1_q1 = [quantize_w1("w1_01", w1_raw[0, 1])]
         a0.extend(rows_a(w1_q0, t) for t in range(2))
-        w1_q1.append(quantize_w1("w1_11", load_w1(1, 1)))
+        w1_q1.append(quantize_w1("w1_11", w1_raw[1, 1]))
         for t in range(2, PACK):
             b0.append(rows_b(0, t))
             e0.append(rows_e(0, t))
@@ -275,7 +285,8 @@ def tile_list_airdata_median_vote_kernel(
                 else:
                     nc.scalar.copy(dst, src)
                 nc.vector.quantize_mx(out=y_codes[:, g, cols].bitcast(FP8X4), scales=y_plane[:, g, cols], in_=y_grouped[:])
-                nc.sync.dma_start(words_view(out_1[g, :, cols, :]), y_codes[:, g, cols].bitcast(I32))
+                if last:
+                    nc.sync.dma_start(words_view(out_1[g]), y_codes[:, g, :].bitcast(I32))
             j0 = j0 + width
         for q in range(4):
             nc.scalar.dma_start(

@@ -126,13 +126,13 @@ def tile_list_airdata_median_vote_kernel(
             tab2_w = load_words("tab2_w", tab2_words[0])
             load_scales(tab3_plane, tab3_scales, 0, nc.sync)
             tab3_w = load_words("tab3_w", tab3_words[0])
+            load_scales(tab_plane, tab_scales, 0, nc.sync)
             w1_raw[0, 0] = load_w1(0, 0, PACK)
             load_scales(w23_plane, w2_scales, 0, nc.sync)
             w2_raw = tables.tile([P, 2 * H], U8, name="w2_raw", align_bytes=64)
             nc.sync.dma_start(w2_raw[:].bitcast(I32), w2_words[0].bitcast(I32))
             w3_raw = load_words("w3_raw", w3_words[0])
             load_scales(w23_plane, w3_scales, 4, nc.sync)
-            load_scales(tab_plane, tab_scales, 0, nc.sync)
             tab_w[0] = load_words("tab_w0", tab_words[0])
             w1_raw[1, 0] = load_w1(1, 0)
             p2 = load_list("p2", pos2)
@@ -272,7 +272,7 @@ def tile_list_airdata_median_vote_kernel(
                 y = late.tile([P, PACK, width], F32, name="late")
                 for t in range(PACK):
                     last_pass(banks[g, t], 1, g, t, z1[0][:], z1[1][:])
-                    if last and t % 2 == 1:
+                    if last and g == 0:
                         nc.vector.tensor_scalar(y[:, t, :], banks[g, t], bias_sb[:, g, t : t + 1], None, ADD)
                     else:
                         nc.scalar.activation(y[:, t, :], banks[g, t], IDENTITY, bias=bias_sb[:, g, t : t + 1])

from contextlib import ExitStack

import concourse.mybir as mybir

K, K2, T, S, H, W, N = 1024, 512, 2048, 1024, 1024, 512, 1024
FLOPS = 2 * (K + 2 * K2) * H * S + 2 * H * N * W

F32 = mybir.dt.float32
BF16 = mybir.dt.bfloat16
I32 = mybir.dt.int32
U32 = mybir.dt.uint32
U16 = mybir.dt.uint16
U8 = mybir.dt.uint8
FP8X4 = mybir.dt.float8_e4m3fn_x4
FP4X4 = mybir.dt.float4_e2m1fn_x4
MIN = mybir.AluOpType.min
MAX = mybir.AluOpType.max
ADD = mybir.AluOpType.add
IDENTITY = mybir.ActivationFunctionType.Identity

P = 128
PACK = 4
GROUP = P * PACK
BANK = 512
BANKS = 8
ON_VECTOR = ["w1_10"]
PARTS = (256, 128, 128)


def tile_list_airdata_median_vote_kernel(
    tc, tab_words, tab_scales, tab2_words, tab2_scales, tab3_words, tab3_scales,
    offs, offs2, offs3, pos1, pos2, pos3,
    w1, w2_words, w2_scales, w3_words, w3_scales, w4, bias,
    out_0, out_1, out_2,
):
    nc = tc.nc
    with ExitStack() as ctx:
        lists = ctx.enter_context(tc.tile_pool(name="lists", bufs=1))
        keep = ctx.enter_context(tc.tile_pool(name="keep", bufs=1))
        raw_pool = ctx.enter_context(tc.tile_pool(name="raw", bufs=4))
        late = ctx.enter_context(tc.tile_pool(name="late", bufs=4))
        stage = ctx.enter_context(tc.tile_pool(name="stage", bufs=2))
        rows = ctx.enter_context(tc.tile_pool(name="rows", bufs=4))
        psum = ctx.enter_context(tc.psum_pool(name="psum", bufs=1))
        with tc.tile_pool(name="tables", bufs=1) as tables:

            def load_list(name, src):
                tile = lists.tile(list(src.shape), U16, name=name)
                nc.sync.dma_start(tile[:], src)
                return tile

            def words_view(ap):
                return ap.rearrange("p c i -> p (c i)").bitcast(I32)

            def load_words(name, src):
                tile = tables.tile([P, src.shape[1]], U32, name=name, align_bytes=64)
                step = 1024
                for c0 in range(0, src.shape[1], step):
                    nc.sync.dma_start(tile[:, c0 : c0 + step].bitcast(I32), words_view(src[:, c0 : c0 + step, :]))
                return tile

            def zeroed_plane(name, width, engine):
                tile = tables.tile([P, width], U8, name=name, align_bytes=64)
                engine.memset(tile[:].bitcast(I32), 0)
                return tile

            def load_scales(tile, src, first_row, queue, quadrants=range(4)):
                passes = src.shape[0]
                for q in quadrants:
                    p0 = 32 * q + first_row
                    queue.dma_start(tile[p0 : p0 + 4 * passes, :].bitcast(I32), src[:, 4 * q : 4 * q + 4, :].bitcast(I32))

            def gather(name, table, offsets, dtype):
                tile = keep.tile([P, S], dtype, name=name, align_bytes=64)
                nc.vector.tensor_copy(tile[:], table[:].indirect(offsets[:]))
                return tile

            def load_w1(a, g, step=2):
                raw = raw_pool.tile([P, PACK, GROUP], F32, name="raw")
                src = w1[a * GROUP : (a + 1) * GROUP, g * GROUP : (g + 1) * GROUP]
                for j in range(0, PACK, step):
                    nc.sync.dma_start(raw[:, j : j + step, :], src.rearrange("(p j) c -> p j c", j=PACK)[:, j : j + step, :])
                return raw

            def load_w4(a, g):
                raw = late.tile([P, PACK, GROUP], F32, name="late")
                src = w4[a * GROUP : (a + 1) * GROUP, g * GROUP : (g + 1) * GROUP].rearrange("(u j i) c -> j u i c", j=PACK, i=4)
                for j in range(PACK):
                    nc.sync.dma_start(raw[:, j, :], src[j])
                return raw

            def quantize(name, grouped, width):
                codes = keep.tile([P, width], U32, name=name + "_codes", align_bytes=64)
                plane = keep.tile([P, width], U8, name=name + "_plane", align_bytes=64)
                nc.vector.quantize_mx(out=codes[:].bitcast(FP8X4), scales=plane[:], in_=grouped)
                return codes, plane

            def quantize_w1(name, raw):
                copy = nc.vector.tensor_copy if name in ON_VECTOR else nc.scalar.copy
                grouped = stage.tile([P, PACK * GROUP], BF16, name="grouped", align_bytes=64)
                copy(
                    grouped[:].rearrange("p (t u i j) -> p u t j i", t=PACK, i=4, j=PACK),
                    raw[:].rearrange("p j (u t i) -> p u t j i", t=PACK, i=4),
                )
                return quantize(name, grouped[:], GROUP)

            def quantize_w4(name, raw):
                copy = nc.vector.tensor_copy if name in ON_VECTOR else nc.scalar.copy
                grouped = stage.tile([P, PACK * GROUP], BF16, name="grouped", align_bytes=64)
                copy(
                    grouped[:].rearrange("p (t m j) -> p m j t", t=PACK, j=PACK),
                    raw[:].rearrange("p j (m t) -> p m j t", t=PACK),
                )
                return quantize(name, grouped[:], GROUP)

            tab2_plane = zeroed_plane("tab2_plane", T, nc.vector)
            tab3_plane = zeroed_plane("tab3_plane", T, nc.vector)
            w23_plane = zeroed_plane("w23_plane", H, nc.vector)
            tab_plane = zeroed_plane("tab_plane", T, nc.vector)

            w1_raw, tab_w = {}, {}
            idx2 = load_list("idx2", offs2)
            idx3 = load_list("idx3", offs3)
            idx = load_list("idx", offs)
            load_scales(tab2_plane, tab2_scales, 0, nc.sync)
            tab2_w = load_words("tab2_w", tab2_words[0])
            load_scales(tab3_plane, tab3_scales, 0, nc.sync)
            tab3_w = load_words("tab3_w", tab3_words[0])
            load_scales(tab_plane, tab_scales, 0, nc.sync)
            w1_raw[0, 0] = load_w1(0, 0, PACK)
            load_scales(w23_plane, w2_scales, 0, nc.sync)
            w2_raw = tables.tile([P, 2 * H], U8, name="w2_raw", align_bytes=64)
            nc.sync.dma_start(w2_raw[:].bitcast(I32), w2_words[0].bitcast(I32))
            w3_raw = load_words("w3_raw", w3_words[0])
            load_scales(w23_plane, w3_scales, 4, nc.sync)
            tab_w[0] = load_words("tab_w0", tab_words[0])
            w1_raw[1, 0] = load_w1(1, 0)
            p2 = load_list("p2", pos2)
            p3 = load_list("p3", pos3)
            tab_w[1] = load_words("tab_w1", tab_words[1])
            w1_raw[0, 1] = load_w1(0, 1)
            w1_raw[1, 1] = load_w1(1, 1)
            p1 = load_list("p1", pos1)
            bias_sb = keep.tile([P, 2, PACK], F32, name="bias_sb")
            nc.sync.dma_start(bias_sb[:], bias.rearrange("(g p t) -> p g t", p=P, t=PACK))

            v2_plane = gather("v2_plane", tab2_plane, idx2, U8)
            v2_w = gather("v2_w", tab2_w, idx2, U32)
            v3_plane = gather("v3_plane", tab3_plane, idx3, U8)
            v3_w = gather("v3_w", tab3_w, idx3, U32)
            def deal(name, raw, dtype, width, run):
                dealt = keep.tile([P, width], dtype, name=name, align_bytes=64)
                nc.vector.tensor_copy(
                    dealt[:].bitcast(I32).rearrange("p (g t u h) -> p g u t h", g=2, t=PACK, h=run),
                    raw[:].bitcast(I32).rearrange("p (g u t h) -> p g u t h", g=2, t=PACK, h=run),
                )
                return dealt

            w2_dealt = deal("w2_dealt", w2_raw, U8, 2 * H, 2)
            w3_dealt = deal("w3_dealt", w3_raw, U32, H, 4)
            w23_dealt = deal("w23_dealt", w23_plane, U8, H, 1)
            v_plane = gather("v_plane", tab_plane, idx, U8)
            v_w = [gather("v_w%d" % a, tab_w[a], idx, U32) for a in range(2)]
        picks = ctx.enter_context(tc.tile_pool(name="picks", bufs=1))

        bank_count = [0]

        def next_bank():
            tile = psum.tile([P, BANK], F32, name="bank%d" % (bank_count[0] % BANKS))
            bank_count.append(bank_count.pop() + 1)
            return tile

        def first_stage(name, passes):
            result = rows.tile([P, S], F32, name=name)
            for c0 in range(0, S, BANK):
                cols = slice(c0, c0 + BANK)
                bank = next_bank()
                for i, (lhsT, lhsT_scale, words, plane, row) in enumerate(passes):
                    nc.tensor.matmul_mx(
                        out=bank[:], lhsT=lhsT, lhsT_scale=lhsT_scale,
                        rhs=words[:, cols].bitcast(FP8X4), rhs_scale=plane[row:P, cols],
                        start=(i == 0), stop=(i == len(passes) - 1),
                    )
                nc.scalar.copy(result[:, cols], bank[:])
            return result

        def rows_b(g, t):
            c = (g * PACK + t) * P
            return first_stage("b", [(w2_dealt[:, 2 * c : 2 * (c + P)].bitcast(FP4X4), w23_dealt[:, c : c + P], v2_w, v2_plane, 0)])

        def rows_e(g, t):
            c = (g * PACK + t) * P
            return first_stage("e", [(w3_dealt[:, c : c + P].bitcast(FP8X4), w23_dealt[4:P, c : c + P], v3_w, v3_plane, 0)])

        def rows_a(w1_q, t):
            cols = slice(t * P, (t + 1) * P)
            return first_stage("a", [(w1_q[a][0][:, cols].bitcast(FP8X4), w1_q[a][1][:, cols], v_w[a], v_plane, 4 * a) for a in range(2)])

        work = [picks.tile([P, PACK * W], F32, name="work%d" % i) for i in range(5)]

        def pick(x, at, source, positions, j0, width):
            nc.vector.tensor_copy(x[:, at : at + width], source[:].indirect(positions[:, j0 // 16 : (j0 + width) // 16]))

        def vote(name, a, b, e, tiles, j0, width):
            base = 0
            x1, x2, x3, high, low = tiles
            for t in range(PACK):
                pick(x2, base + t * width, b[t], p2, j0, width)
                pick(x3, base + t * width, e[t], p3, j0, width)
                pick(x1, base + t * width, a[t], p1, j0, width)
                if t % 2 == 1:
                    cols = slice(base + (t - 1) * width, base + (t + 1) * width)
                    nc.vector.tensor_tensor(high[:, cols], x1[:, cols], x2[:, cols], MAX)
                    nc.vector.tensor_tensor(low[:, cols], x1[:, cols], x2[:, cols], MIN)
                    nc.vector.tensor_tensor(high[:, cols], high[:, cols], x3[:, cols], MIN)
            cols = slice(base, base + PACK * width)
            z = stage.tile([P, PACK * width], BF16, name="z", align_bytes=64)
            nc.vector.tensor_tensor(
                z[:].rearrange("p (c i t) -> p c t i", i=4, t=PACK),
                low[:, cols].rearrange("p (t c i) -> p c t i", i=4, t=PACK),
                high[:, cols].rearrange("p (t c i) -> p c t i", i=4, t=PACK),
                MAX,
            )
            return quantize(name, z[:], width)

        w1_q0 = [quantize_w1("w1_%d0" % a, w1_raw[a, 0]) for a in range(2)]
        a0, b0, e0 = [], [], []
        for t in range(2):
            b0.append(rows_b(0, t))
            e0.append(rows_e(0, t))
        w1_q1 = [quantize_w1("w1_01", w1_raw[0, 1])]
        a0.extend(rows_a(w1_q0, t) for t in range(2))
        w1_q1.append(quantize_w1("w1_11", w1_raw[1, 1]))
        for t in range(2, PACK):
            b0.append(rows_b(0, t))
            e0.append(rows_e(0, t))
            a0.append(rows_a(w1_q0, t))
        z0 = vote("z0", a0, b0, e0, work, 0, W)

        a1, b1, e1 = [], [], []
        w4_q = {}
        for t in range(PACK):
            if t < 3:
                w4_q[t // 2, t % 2] = quantize_w4("w4_%d" % t, load_w4(t // 2, t % 2))
            b1.append(rows_b(1, t))
            e1.append(rows_e(1, t))
            a1.append(rows_a(w1_q1, t))
        w4_q[1, 1] = quantize_w4("w4_3", load_w4(1, 1))

        y_codes = keep.tile([P, 2, W], U32, name="y_codes", align_bytes=64)
        y_plane = keep.tile([P, 2, W], U8, name="y_plane", align_bytes=64)

        def last_pass(bank, a, g, t, codes, plane):
            cols = slice(t * P, (t + 1) * P)
            nc.tensor.matmul_mx(
                out=bank, lhsT=w4_q[a, g][0][:, cols].bitcast(FP8X4), lhsT_scale=w4_q[a, g][1][:, cols],
                rhs=codes.bitcast(FP8X4), rhs_scale=plane, start=(a == 0), stop=(a == 1),
            )

        j0 = 0
        for width in PARTS:
            cols = slice(j0, j0 + width)
            last = j0 + width == W
            banks = {}
            for g in range(2):
                for t in range(PACK):
                    banks[g, t] = next_bank()[:, :width]
                    last_pass(banks[g, t], 0, g, t, z0[0][:, cols], z0[1][:, cols])
            z1 = vote("z1_%d" % j0, a1, b1, e1, work, j0, width)
            work = [work[0], work[3], work[4], work[1], work[2]]
            for g in range(2):
                y = late.tile([P, PACK, width], F32, name="late")
                for t in range(PACK):
                    last_pass(banks[g, t], 1, g, t, z1[0][:], z1[1][:])
                    if last and g == 0:
                        nc.vector.tensor_scalar(y[:, t, :], banks[g, t], bias_sb[:, g, t : t + 1], None, ADD)
                    else:
                        nc.scalar.activation(y[:, t, :], banks[g, t], IDENTITY, bias=bias_sb[:, g, t : t + 1])
                nc.sync.dma_start(out_0[g * GROUP : (g + 1) * GROUP, cols].rearrange("(p t) j -> p t j", t=PACK), y[:])
                y_grouped = stage.tile([P, PACK * width], BF16, name="grouped", align_bytes=64)
                dst = y_grouped[:].rearrange("p (c i t) -> p c t i", i=4, t=PACK)
                src = y[:].rearrange("p t (c i) -> p c t i", i=4)
                if last:
                    nc.vector.tensor_copy(dst, src)
                else:
                    nc.scalar.copy(dst, src)
                nc.vector.quantize_mx(out=y_codes[:, g, cols].bitcast(FP8X4), scales=y_plane[:, g, cols], in_=y_grouped[:])
                if last:
                    nc.sync.dma_start(words_view(out_1[g]), y_codes[:, g, :].bitcast(I32))
            j0 = j0 + width
        for q in range(4):
            nc.scalar.dma_start(
                out_2[:, 4 * q : 4 * q + 4, :].bitcast(I32).rearrange("g r c -> r g c"),
                y_plane[32 * q : 32 * q + 4, :, :].bitcast(I32),
            )
